import numpy as np, ml_dtypes
CORES = [35,38,43,46]
N = 4
BF = ml_dtypes.bfloat16
L, M, P, RO = 256, 1024, 1, 5
PLANT = [[139, 0, 0], [849, 0, 1], [958, 1, 0], [848, 0, 0]]
LIMS = [[0, 2], [3, 1]]
BRINK = 143
def skew(rng):
    return np.minimum((M * rng.random((N, 8, 16, L)) ** rng.choice(np.array([0.5, 1.0, 2.0]), (N, 8, 16, 1))).astype(np.int64), M - 1)
def parts(rng):
    col = skew(rng); om = np.where(rng.random((N, 8, 16, L)) < rng.choice(np.array([0.4, 0.7, 0.95]), (N, 8, 1, 1)), skew(rng), 0)
    who = np.minimum((16 * rng.random((N, 8, L)) ** rng.choice(np.array([1.5, 2.0, 3.0]), (1, 8, 1))).astype(np.int64), 15)
    order = np.argsort(rng.random((8, 16)), axis=1); mem = order[np.arange(8)[None, :, None], who]
    th = np.minimum(np.maximum(rng.permutation(np.array([1, 2, 3, 4, 6, 8, 9, 11]))[None, :] + rng.integers(-1, 2, (N, 8)), 1), 16)
    return col, om, mem, th
def pack(col, om, mem, th):
    return {"col": np.ascontiguousarray(col.reshape(N, 128, L)).astype(np.int32), "om": np.ascontiguousarray(om.reshape(N, 128, L)).astype(np.int32),
            "mem": np.ascontiguousarray(mem).astype(np.int32), "th": np.ascontiguousarray(th.reshape(N, 8, 1)).astype(np.int32)}
def near(rng, g, col, om, mem, th):
    s = int(rng.integers(0, N)); b = rng.permutation(16)
    col[:, g] = np.maximum(skew(rng)[:, g], 1); om[:, g] = 0; mem[:, g] = b[rng.integers(3, 16, (N, L))]
    for n, k, c in PLANT:
        r, i = (n // L + s) % N, n % L
        mem[r, g, i] = b[k]; om[r, g, b[(k + np.arange(c)) % 16], i] = 1
    for r, v in LIMS: th[(r + s) % N, g] = v
def brink(rng, g, col, om, mem, th):
    b = rng.permutation(16); r, i = BRINK // L, BRINK % L; v = rng.integers(1, M - 1, 2)
    col[:, g] = np.minimum(col[:, g], M - 2); col[:, g, b[2:4]] = 0; col[N - 1, g, b[2:4], L - 1] = v
    om[:, g] = 0; om[r, g, b[2:4], i] = rng.integers(1, v + 1)
    mem[:, g] = b[0]; mem[r, g, i] = b[1]; th[r, g] = 2
def setup_inputs(rng):
    return pack(*parts(rng))
def setup_inputs_lone(rng):
    col, om, mem, th = parts(rng)
    for g in (0, 2, 4, 6): mem[:, g] = rng.integers(0, 16)
    for g in (1, 5): mem[:, g] = ((np.arange(N) + rng.integers(0, 16)) & 15)[:, None]
    a, b = rng.permutation(16)[:2]
    mem[:, 3] = np.where(mem[:, 3] == a, b, mem[:, 3]); mem[N - 1, 3, L - 1] = a
    mem[:, 7] = np.where(mem[:, 7] == b, a, mem[:, 7]); mem[0, 7, 0] = b
    return pack(col, om, mem, th)
def setup_inputs_ties(rng):
    col, om, mem, th = parts(rng)
    v = rng.integers(1, M - 1, (8, 6)); v[:, 0] = 0; v[:, 1] = M - 1; g = np.arange(8)[None, :, None, None]
    col = v[g, rng.integers(0, 6, (N, 8, 16, L))]; om = v[g, rng.integers(0, 6, (N, 8, 16, L))]
    near(rng, int(rng.integers(0, 8)), col, om, mem, th)
    return pack(col, om, mem, th)
def setup_inputs_ends(rng):
    col, om, mem, th = parts(rng); q = rng.permutation(8); th = rng.integers(1, 17, (N, 8))
    col[:, q[:3]] = np.maximum(col[:, q[:3]], 1); om[:, q[:3]] = 1
    om[:, q[1], rng.integers(0, 16)] = 0; om[:, q[2], rng.integers(0, 16)] = 0
    th[:, q[0]] = 16; th[:, q[1]] = 16; th[:, q[2]] = 15; th[rng.integers(0, N), q[1]] = 1
    om[:, q[3]] = 0; th[:, q[3]] = 1; om[:, q[4]] = M - 1; col[:, q[4], ::3] = M - 1; th[:, q[4]] = rng.integers(1, 4, N); th[:, q[5]] = 1
    k, j = rng.permutation(16)[:2]; v = int(rng.integers(1, M - 1))
    c = np.maximum(col[:, q[6]], 1); c = np.where(c == v, v + 1, c); c[:, k] = v; c[v // L, j, v % L] = 0
    col[:, q[6]] = c; om[:, q[6]] = 1; th[:, q[6]] = 16
    brink(rng, int(q[7]), col, om, mem, th)
    return pack(col, om, mem, th)
def setup_inputs_far(rng):
    col, om, mem, th = parts(rng)
    col[:, ::2] = ((np.arange(N) + 1) % N * L)[:, None, None, None] + rng.integers(0, L, (N, 4, 16, L))
    col[:, 1] = rng.integers(0, 16, (N, 16, L)); col[:, 5] = rng.integers(0, 16, (N, 16, L))
    for g in (0, 1, 4, 5): mem[:, g] = rng.permutation(16)[:2][rng.integers(0, 2, (N, L))]
    return pack(col, om, mem, th)
def setup_inputs_spread(rng):
    col, om, mem, th = parts(rng); h = np.log2(M)
    col = np.minimum((np.exp2(h * rng.random((N, 8, 1, L)) ** 0.5) * rng.random((N, 8, 16, L))).astype(np.int64), M - 1)
    om = np.minimum((np.exp2(h * rng.random((N, 8, 16, L))) - 1).astype(np.int64), M - 1)
    th = np.minimum(np.exp2(4.1 * rng.random((N, 8))).astype(np.int64), 16); th[:, rng.integers(0, 8)] = 1
    return pack(col, om, mem, th)
def check_inputs(d):
    bad = []
    for k, lo, hi in (("col", 0, M - 1), ("om", 0, M - 1), ("mem", 0, 15), ("th", 1, 16)):
        if np.min(d[k]) < lo or np.max(d[k]) > hi: bad.append("range of " + k)
    return bad
def reference(col, om, mem, th):
    def joined(a): return np.ascontiguousarray(a.astype(np.int64).reshape(N, 8, 16, L).transpose(1, 2, 0, 3)).reshape(8, 16, M)
    def parted(a): return np.ascontiguousarray(a.reshape(8, 16, N, L).transpose(2, 0, 1, 3)).reshape(N, 128, L)
    vec = np.zeros((8, 16, M * (RO + 1)), np.int64); vec[:, :, :M] = joined(col)
    w = joined(om); R = np.zeros((8, M), np.int64); S = np.zeros((8, M), np.int64)
    one = mem.astype(np.int64).transpose(1, 0, 2).reshape(8, 1, M) == np.arange(16)[None, :, None]
    lim = np.repeat(th.astype(np.int64)[:, :, 0].T, L, axis=1); lane = np.arange(M); i = np.tile(np.arange(L), N); none = 2 ** 20
    hist = []
    for t in range(RO):
        last = vec[:, :, M * t:M * (t + 1)]; e = M * (t + 1) + lane
        par = [(last, w, R)]
        for p in range(P):
            o = (5 * i + (lane - i) + 61 * S + 16 * R + 77 * t + 341 * p) & (M - 1)
            par.append((np.take_along_axis(last, o[:, None, :], 2), np.take_along_axis(w, o[:, None, :], 2), np.take_along_axis(R, o, 1)))
        x = np.where(one, e, np.maximum.reduce([a[0] for a in par]))
        vec[:, :, M * (t + 1):M * (t + 2)] = x
        top = np.maximum.reduce([a[2] for a in par])
        low = np.minimum.reduce([np.where((a[2] == top)[:, None, :] & (a[1] > 0), a[1], none) for a in par])
        c = np.zeros((8, 16, M), np.int64)
        for k in range(16):
            c += np.take_along_axis(vec, x[:, k:k + 1, :], 2) >= low
        S = np.add.reduce((c >= lim[:, None, :]).astype(np.int64), axis=1)
        up = S >= lim; R = top + up
        w = np.where(up[:, None, :], np.where(one, e, 0), np.where(low == none, 0, low))
        hist.append(R)
    yr = np.ascontiguousarray(np.stack(hist).reshape(RO, 8, N, L).transpose(2, 1, 0, 3)).reshape(N, 8, RO * L)
    return {"yx": parted(x).astype(np.float32), "yo": parted(w).astype(np.float32), "yr": yr.astype(np.float32)}

from concourse.bass import DstId, RemoteDMATransfer
from concourse.mybir import AluOpType as A, ActivationFunctionType as AF

L, H, M, RO = 256, 128, 1024, 5
EV = RO * L
KB = 8192
C0 = KB * 128
RS, RB = -1.0 / KB, -(0.5 + 1.0 / 16384)
CFG = {"rep": 4, "chunks": [(64, 128), (0, 64)], "gchunks": [(64, 128), (0, 64)],
       "splitx": False, "splitp": False, "splitk": False, "rfA": "V", "rfT": "S", "q": "S",
       "cyc": 1.04, "gam": 1.56, "pe": 0.52, "fix": 60, "hop": 100, "link": 55.0, "row": 30.0,
       "lat": 1000, "first": 2000, "slack": 20}
BIAS = {"e1P": 500, "e1V": 2500, "e1S": 12500, "b1V": 11000, "b1S": 12500, "b1P": 18000, "f1V": 14500, "e0P": 2500,
        "e0V": 12500, "e0S": 7500, "f0V": 2000, "c1P": 7500, "b0P": -2000, "rP": -11500, "rS": -5500, "f0S": 10500,
        "sV": -1000, "u1P": -500, "b0S": -14500, "k1V": 7500, "sS": 6000, "u0V": -3500, "f1S": 21000, "sP": -10000,
        "k0P": -3000, "k1P": 4000, "u0P": 3000, "u1V": -9000, "c0P": -1500, "sG": 3000, "b0V": -5500, "c0V": -2000}
REP = CFG["rep"]

F32, BF, I32, U16 = "float32", "bfloat16", "int32", "uint16"
SCRATCH = {}
for _dt, _bufs in (
        (I32, {"ci": L, "oi": L, "mt": 264, "ic": 4, "w3": 16, "w4": 16}),
        (U16, {"off": L, "ou": 16}),
        (F32, {"U": 144, "Un": L, "I16": 128, "fc": 16, "BT": 80, "BT2": 80, "NI": 128, "t1": L, "t2": L, "t3": L, "t4": L,
               "W": EV + RO * M, "KK": RO * M, "KP": RO * M, "XS": RO * L, "KA": L, "KS": RO * L, "tmp": L, "G": 16 * L,
               "Ro": RO * L, "yb": L}),
        (BF, {"mtb": 264, "Id": 128, "M8": 128, "D": 640, "E": 640, "Q3": 384, "Fw": 144, "BO": 128, "EX": 128, "Sel": 16,
              "one": L, "Bn": L, "CK": L, "thB": 4 * L, "thG": 4 * L, "rfA": L, "rfT": L, "C": 16 * L,
              "good": L, "bad": L, "ge": L, "sg": L, "q": L})):
    for _n in _bufs:
        SCRATCH[_n] = ("sbuf", [128, _bufs[_n]], _dt)
PSUM = ("pc0", "pc1", "pl0", "pl1", "pT", "pU", "pS", "pw")
for _n in PSUM:
    SCRATCH[_n] = ("psum", [128, 512], F32)
ND, NX = 40, 26
SEMAPHORES = (["eV", "eS", "eP", "eG"] + ["d%d" % k for k in range(ND)]
              + ["xl%d" % k for k in range(NX)] + ["xa%d" % k for k in range(NX)])


def lanes_to(topo, src, dsts):
    far = [d for d in dsts if topo.chip(d) != topo.chip(src)]
    near = [d for d in dsts if topo.chip(d) == topo.chip(src)]
    out, used = {}, []
    for n, d in enumerate(far):
        e = topo.engines(src, d)
        k = len(e) // len(far)
        out[d] = e[n * k:(n + 1) * k]
        used += out[d]
    for n, d in enumerate(near):
        e = [x for x in topo.engines(src, d) if x not in used]
        k = len(e) // len(near)
        out[d] = e[n * k:(n + 1) * k]
    return out


def hits(xs, ys):
    for a in xs:
        for b in ys:
            if a[0] == b[0] and a[1] < b[2] and b[1] < a[2]:
                return True
    return False


def depends(ops):
    by, deps = {}, []
    for n, o in enumerate(ops):
        names = set(a[0] for a in o["r"] + o["w"])
        mine = set(o.get("after", []))
        if o["q"] is not None:
            for m in set(m for x in names for m in by.get(x, [])):
                p = ops[m]
                same = p["kind"] == "c" and o["kind"] == "c" and p["q"] == o["q"]
                if hits(o["r"], p["w"]) or hits(o["w"], p["w"]) or hits(o["w"], p["r"]):
                    mine.add(m)
                elif (not same or o["q"] == "P") and any(x in PSUM and x in p["names"] for x in names):
                    mine.add(m)
        o["names"] = names
        for x in names:
            by.setdefault(x, []).append(n)
        deps.append(mine)
    return deps


def schedule(ops, deps):
    n, hop = len(ops), CFG["hop"]
    nxt = [[] for _ in ops]
    for i in range(n):
        for m in deps[i]:
            nxt[m].append(i)
    path = [0.0] * n
    for i in range(n - 1, -1, -1):
        path[i] = ops[i]["t"] + ops[i]["lat"] + max([path[j] + (0 if ops[i]["q"] == ops[j]["q"] == "P" else hop) for j in nxt[i]] + [0])
    prio = [path[i] - ops[i]["t"] + BIAS.get(ops[i].get("tag"), 0) for i in range(n)]
    left, est, free, link, order = [len(d) for d in deps], [0.0] * n, {}, [0.0, True], []
    ready = [i for i in range(n) if left[i] == 0]
    while ready:
        at = dict((i, max(est[i], free.get(ops[i]["q"], 0.0)) if ops[i]["q"] else -1.0) for i in ready)
        i0 = min(ready, key=lambda i: (at[i], i))
        i = max((j for j in ready if ops[j]["q"] == ops[i0]["q"] and at[j] <= at[i0] + CFG["slack"]), key=lambda j: (prio[j], -j))
        ready.remove(i)
        order.append(i)
        o = ops[i]
        if o["q"] is None:
            done = est[i] - hop
        else:
            free[o["q"]] = at[i] + o["t"]
            done = at[i] + o["t"] + o["lat"]
            if o["kind"] == "x":
                link[0] = max(link[0], at[i] + o["t"] + CFG["lat"] + (CFG["first"] if link[1] else 0)) + o["lat"] - 2 * CFG["lat"]
                link[1] = False
                done = link[0] + CFG["lat"]
        for j in nxt[i]:
            est[j] = max(est[j], done + (0 if o["q"] == ops[j]["q"] == "P" else hop))
            left[j] -= 1
            if left[j] == 0:
                ready.append(j)
    return order


def emit(g, T, ops):
    queue = {"V": g.vector, "S": g.scalar, "P": g.tensor, "G": g, "Y": g.sync}
    deps = depends(ops)
    order = schedule(ops, deps)
    place = dict((i, k) for k, i in enumerate(order))
    seen, need = {}, {}
    for i in order:
        o, last = ops[i], {}
        for m in (deps[i] if o["q"] else []):
            p = ops[m]
            if p["q"] == o["q"] == "P":
                continue
            key = p["q"] if p["kind"] == "c" else m
            if place[m] > last.get(key, (-1, 0))[0]:
                last[key] = (place[m], m)
        need[i] = []
        for key in last:
            if seen.get((o["q"], key), -1) < last[key][0]:
                seen[(o["q"], key)] = last[key][0]
                need[i].append(last[key][1])
    wanted = set(m for i in order for m in need[i])
    count = {"V": 0, "S": 0, "P": 0, "G": 0}
    for i in order:
        o = ops[i]
        if o["kind"] == "c" and i in wanted:
            count[o["q"]] += 1
            o["sem"], o["val"] = "e" + o["q"], count[o["q"]]
    for i in order:
        o = ops[i]
        if o["q"] is None:
            continue
        for m in need[i]:
            queue[o["q"]].wait_ge(T.sem[ops[m]["sem"]], ops[m]["val"])
        ins = o["f"](queue[o["q"]])
        if o["kind"] == "c" and i in wanted:
            ins.then_inc(T.sem[o["sem"]], 1)
        if o["kind"] == "d":
            ins.then_inc(T.sem[o["sem"]], 16)
    for i in order:
        if ops[i]["kind"] != "c" and i not in wanted:
            g.wait_ge(T.sem[ops[i]["sem"]], ops[i]["val"])


def rank_program(g, core, T, topo):
    r = T.rank_of(core)
    if r is None:
        return
    cores = list(T.cores)
    peers = [c for c in cores if c != core]
    eng = lanes_to(topo, core, peers)
    n_out = sum(len(e) for e in eng.values())
    n_in = sum(len(lanes_to(topo, s, [c for c in cores if c != s])[core]) for s in peers)
    ops, nd, nx, cur = [], [0], [0], ["s"]

    def op(q, f, rd, wr, cycles):
        t = cycles * CFG["pe"] if q == "P" else max(64, cycles) * CFG["cyc"] + CFG["fix"]
        ops.append({"q": q, "kind": "c", "f": f, "r": rd, "w": wr, "t": t, "lat": 0, "tag": cur[0] + q})

    def dma(q, out, in_, rd, wr, add=False):
        f = (lambda e: e.dma_start(out, in_, accum_op=A.add)) if add else (lambda e: e.dma_start(out, in_))
        ops.append({"q": q, "kind": "d", "f": f, "r": rd, "w": wr, "sem": "d%d" % nd[0], "val": 16,
                    "t": 1000 if q == "G" else 60, "lat": 2400})
        nd[0] += 1

    def share(sname, s0, dname, d0, a, b):
        k = nx[0]
        nx[0] += 1

        def f(e):
            trs = []
            for d in peers:
                ad = topo.addr(d)
                trs.append(RemoteDMATransfer(dst_ids=[DstId(rid=ad[0], pnc=ad[1])], dma_engine_mask=sum(1 << x for x in eng[d]),
                                             remote_sem=T.sem["xa%d" % k], src=T[sname][:, s0 + a:s0 + b],
                                             dst=T[dname][:, d0 + L * r + a:d0 + L * r + b]))
            return e.remote_dma_fused(trs, local_sem=T.sem["xl%d" % k])
        ops.append({"q": "G", "kind": "x", "f": f, "r": [(sname, s0 + a, s0 + b)], "w": [], "sem": "xl%d" % k, "val": n_out,
                    "t": 200, "lat": 2 * CFG["lat"] + 32 * (CFG["row"] + CFG["link"] * (b - a) / L)})
        ops.append({"q": None, "kind": "a", "r": [], "after": [len(ops) - 1], "t": 0, "lat": 0, "sem": "xa%d" % k, "val": n_in,
                    "w": [(dname, d0 + L * s + a, d0 + L * s + b) for s in range(len(cores)) if s != r]})

    def share_half(split, h, sname, s0, dname, d0):
        if split:
            share(sname, s0, dname, d0, H * h, H * h + H)
        elif h == 0:
            share(sname, s0, dname, d0, 0, L)

    def v(name, a=None, b=None, rows=128, step=1):
        if a is None:
            a, b = 0, T[name].shape[1]
        return (T[name][0:rows, a:b:step] if step > 1 else T[name][0:rows, a:b], name, a, b, (b - a + step - 1) // step)

    def col(k, rows=128):
        return v("fc", k, k + 1, rows)

    def rg(*xs):
        return [x[1:4] for x in xs if isinstance(x, tuple)]

    def ap(x):
        return x[0] if isinstance(x, tuple) else x

    def narrow(*xs):
        return all(x[1] in SCRATCH and SCRATCH[x[1]][2] in (BF, U16) for x in xs)

    def ind(win, offs):
        return win[0].indirect(offs[0])

    def ts(out, in0, s1, s2, o0, o1=None):
        c = out[4] / (2 if narrow(out, in0) else 1)
        if o1 is None:
            op("V", lambda e: e.tensor_scalar(out[0], in0[0], ap(s1), None, o0), rg(in0, s1), rg(out), c)
        else:
            op("V", lambda e: e.tensor_scalar(out[0], in0[0], ap(s1), ap(s2), o0, o1), rg(in0, s1, s2), rg(out), c)

    def tt(out, in0, in1, o):
        op("V", lambda e: e.tensor_tensor(out[0], in0[0], in1[0], o), rg(in0, in1), rg(out),
           out[4] * (1 if in0[1] in PSUM or in1[1] in PSUM else 2))

    def ttg(out, win, offs, in1, o):
        op("V", lambda e: e.tensor_tensor(out[0], ind(win, offs), in1[0], o), rg(win, offs, in1), rg(out), out[4] * CFG["gam"])

    def cp(out, in_):
        op("V", lambda e: e.tensor_copy(out[0], in_[0]), rg(in_), rg(out), out[4])

    def act(out, in_, func, bias=0.0, scale=1.0):
        op("S", lambda e: e.activation(out[0], in_[0], func, bias=ap(bias), scale=scale), rg(in_, bias), rg(out), out[4])

    def mm(out, lhsT, rhs, start, stop):
        op("P", lambda e: e.matmul(out[0], lhsT[0], rhs[0], start, stop), rg(lhsT, rhs), rg(out),
           max(min(64, lhsT[4]), rhs[4]) * (4 if lhsT[1] == "NI" else 1))

    def iota(out, pat, base, cm, flt=True):
        if flt:
            op("G", lambda e: e.iota(out[0], pat, base, cm, allow_small_or_imprecise_dtypes=True), [], rg(out), 70 + 2 * out[4])
        else:
            op("G", lambda e: e.iota(out[0], pat, base, cm), [], rg(out), 70 + 2 * out[4])

    def rounded(q, out, key):
        if q == "S":
            act(out, key, AF.Identity, RB, RS)
        else:
            ts(out, key, RS, RB, A.mult, A.add)

    cP, cJ, cG, c16, cJ5, cTH, cSG, cA1, cA2, cAD = range(10)
    own = L * r

    dma("Y", T.ci[:], T.col[:], [], rg(v("ci")))
    dma("S", T.oi[:], T.om[:], [], rg(v("oi")))
    dma("Y", T.mt[0:8, 0:L], T.mem[:], [], rg(v("mt", 0, L)))
    dma("S", T.mt[0:8, L:L + 1], T.th[:], [], rg(v("mt", L, L + 1)))
    cp(v("W", EV + own, EV + own + L), v("ci"))
    share("W", EV + own, "W", EV, 0, L)
    ts(v("t1"), v("oi"), 0.0, float(KB), A.is_gt, A.mult)
    ts(v("t2"), v("oi"), -1.0, float(C0), A.mult, A.add)
    tt(v("KS", 0, L), v("t1"), v("t2"), A.add)
    share("KS", 0, "KK", 0, 0, L)
    dma("Y", T.KK[:, own:own + L], T.KS[:, 0:L], rg(v("KS", 0, L)), rg(v("KK", own, own + L)))
    iota(v("ic", 0, 1), [[0, 1]], 0, 1, False)
    iota(v("I16"), [[16, 8], [0, 16]], 0, 0)
    iota(v("U"), [[1, 144]], 0, 0)
    iota(v("BT"), [[77, RO], [80, 16]], own - 16 * 129, 0)
    iota(v("Un"), [[-1, L]], 0, 0)
    cp(col(cP), v("ic", 0, 1))
    ts(v("ic", 1, 2), v("ic", 0, 1), 15, None, A.bitwise_and)
    ts(col(c16), col(cP), 16.0, None, A.mult)
    cp(col(cJ), v("ic", 1, 2))
    tt(col(cG), col(cP), col(cJ), A.subtract)
    ts(col(cJ5), col(cJ), 5.0, None, A.mult)
    ts(v("EX", rows=8), v("I16", rows=8), col(c16, 8), None, A.is_equal)
    ts(v("BO"), v("I16"), col(cG), None, A.is_equal)
    cp(v("mtb", 0, L + 1, 8), v("mt", 0, L + 1, 8))
    mm(v("pS", 0, L + 1), v("EX", rows=8), v("mtb", 0, L + 1, 8), True, True)
    ts(v("one"), v("pS", 0, L), col(cJ), None, A.is_equal)
    cp(col(cTH), v("pS", L, L + 1))
    ts(v("BT2"), v("BT"), col(cJ5), None, A.add)
    ts(v("w3"), v("BT2", 0, 16), float(16 * 129), None, A.add)
    ts(v("w4"), v("w3"), M - 1, None, A.bitwise_and)
    cp(v("ou"), v("w4"))
    ts(v("Id"), v("U", 0, 128), col(cP), None, A.is_equal)
    ts(v("NI"), v("U", 0, 128), col(cP), -1.0, A.is_equal, A.mult)
    ts(v("M8"), v("Id"), float(-KB), None, A.mult)
    for t in range(RO):
        ts(v("D", 128 * t, 128 * t + 128), v("Id"), float(KB - M * (t + 1) - own), None, A.mult)
        ts(v("E", 128 * t, 128 * t + 128), v("Id"), float((M + L) * (t + 1) + own), None, A.mult)
    ts(v("Q3", 0, 128), v("Id"), 30.5, None, A.mult)
    ts(v("Q3", 128, 256), v("Id"), -1.0, None, A.mult)
    ts(v("Q3", 256, 384), v("Id"), -0.5, None, A.mult)
    ts(v("Fw", 0, 143), v("U", 0, 143), -15.0, col(cG), A.add, A.is_equal)
    ts(v("Sel", 0, 8), v("I16", 0, 128, step=16), col(cP), -1.0, A.is_equal, A.mult)
    ts(v("Sel", 8, 16), v("I16", 0, 128, step=16), col(cP), -0.5, A.is_equal, A.mult)
    tt(v("Bn"), v("one"), v("Un"), A.mult)
    mm(v("pT", 0, L), v("D", 0, 128), v("one"), True, False)
    mm(v("pT", 0, L), v("Id"), v("Bn"), False, False)
    mm(v("pT", 0, L), v("M8"), v("one"), False, True)
    act(v("t3"), v("pT", 0, L), AF.Identity, 0.0, -1.0)
    tt(v("XS", 0, L), v("t3"), v("W", EV + own, EV + own + L), A.max)
    mm(v("pw", L, 2 * L), v("E", 0, 128), v("one"), True, True)
    act(v("XS", L, 2 * L), v("one"), AF.Identity, 0.0, float(M))
    for t in range(2, RO):
        dma("Y", T.XS[:, t * L:(t + 1) * L], T.XS[:, L:2 * L], rg(v("XS", L, 2 * L)), rg(v("XS", t * L, (t + 1) * L)))
    ts(col(cSG), col(cTH), 2.0, -1.0, A.mult, A.add)
    ts(col(cA1), col(cTH), 1.0, None, A.is_le)
    ts(col(cA2), col(cTH), 2.0, None, A.is_le)
    tt(col(cAD), col(cA1), col(cA2), A.subtract)
    ts(v("CK"), v("one"), col(cAD), col(cA2), A.mult, A.add)
    for t in range(1, RO):
        a = (t - 1) * L
        ts(v("thB", a, a + L), v("CK"), float(KB - M * t), float(M * t), A.mult, A.add)
        ts(v("thG", a, a + L), v("CK"), float(M * t - 2 * KB), float(2 * KB), A.mult, A.add)

    def gather(win, a, b):
        offs = v("off", a, b)
        op("S", lambda e: e.activation(T.G[:, 16 * a:16 * b], ind(win, offs), AF.Identity), rg(win, offs), [("G", a, b)],
           16 * (b - a) * CFG["gam"])

    def front(t, h):
        a, b = H * h, H * h + H
        sb = (RO - 1 - t) * L
        cur[0] = "f%d" % h
        x, o = v("W", sb + a, sb + b), v("ou", 8 * h, 8 * h + 8)
        ttg(x, v("W", EV + M * t, EV + M * (t + 1)), o, v("XS", t * L + a, t * L + b), A.max)
        tt(v("tmp", a, b), x, v("pw", L + a, L + b), A.subtract)
        ts(v("off", a, b), v("tmp", a, b), float(L * (t + 1) - a), None, A.add)
        if t == RO - 1:
            dma("Y", T.yx[:, a:b], x[0], rg(x), [])
        else:
            share_half(CFG["splitx"], h, "W", sb, "W", EV + M * (t + 1))
            e = EV + M * (t + 1) + own
            if h == 0:
                xx, xs = v("W", sb, sb + L), v("XS", (t + 1) * L, (t + 2) * L)
                dma("Y", T.W[:, e:e + L], xx[0], rg(xx), rg(v("W", e, e + L)))
                dma("G", xs[0], xx[0], rg(xx, xs), rg(xs), True)
        for c, d in CFG["gchunks"]:
            gather(v("W", sb + a, EV + M * (t + 1)), a + c, a + d)

    def counts(t, h):
        a, b, o = H * h, H * h + H, v("ou", 8 * h, 8 * h + 8)
        cur[0] = "k%d" % h
        kk = v("KS", L * t + a, L * t + b)
        if t == 0:
            ka, rf = v("KP", own + a, own + b), v("rfT", a, b)
            ttg(ka, v("KK", 0, M), o, kk, A.max)
            share_half(CFG["splitp"], h, "KP", own, "KP", 0)
        else:
            ka, rf = v("KA", a, b), v("rfA", a, b)
            ttg(ka, v("KP", M * (t - 1), M * t), o, kk, A.max)
        rounded(CFG["rfA"], rf, ka)
        for k in range(REP):
            out = v("pl%d" % h, k, REP * H, step=REP)
            mm(out, v("NI"), ka, True, False)
            mm(out, v("M8"), rf, False, True)
        cur[0] = "c%d" % h
        st = 16 // REP
        for c, d in CFG["chunks"]:
            for m in range(st):
                k = slice(16 * (a + c) + m, 16 * (a + d), st)
                n = REP * (d - c)
                tt((T.C[:, k], "C%d" % m, a + c, a + d, n), (T.G[:, k], "G", a + c, a + d, n), v("pl%d" % h, REP * c, REP * d), A.is_ge)
        for n, (m, k) in enumerate((m, k) for m in range(st) for k in range(m, 16, st)):
            mm(v("pc%d" % h, 0, H), v("Id"), (T.C[:, 16 * a + k:16 * b:16], "C%d" % m, a, b, H), n == 0, t == 0 and n == 15)

    def back(t, h):
        a, b = H * h, H * h + H
        last = t == RO - 1
        kt, rf, pc = v("KP", M * t + own + a, M * t + own + b), v("rfT", a, b), v("pc%d" % h, 0, H)
        cur[0] = "b%d" % h
        if t > 0:
            ttg(kt, v("KK", M * t, M * (t + 1)), v("ou", 8 * h, 8 * h + 8), v("KS", L * t + a, L * t + b), A.max)
            if not last:
                share_half(CFG["splitp"], h, "KP", M * t + own, "KP", M * t)
            rounded(CFG["rfT"], rf, kt)
            low = v("pT", 0, H)
            mm(low, v("NI"), kt, True, False)
            mm(low, v("M8"), rf, False, True)
            c = (t - 1) * L
            tt(v("good", a, b), low, v("thG", c + a, c + b), A.is_ge)
            tt(v("bad", a, b), low, v("thB", c + a, c + b), A.is_ge)
            mm(pc, v("D", 128 * t, 128 * t + 128), v("good", a, b), False, False)
            mm(pc, v("M8"), v("bad", a, b), False, True)
        if last:
            ts(v("t1", a, b), low, float(KB), 0.5, A.is_lt, A.mult)
            tt(v("t2", a, b), low, v("t1", a, b), A.mult)
            ts(v("t1", a, b), v("W", a, b), float(M * RO), 0.5, A.is_ge, A.mult)
            tt(v("t3", a, b), v("t1", a, b), v("W", a, b), A.mult)
            tt(v("t1", a, b), v("t2", a, b), v("t3", a, b), A.subtract)
            tt(v("t4", a, b), v("t3", a, b), v("t3", a, b), A.add)

    def close(t, h):
        a, b = H * h, H * h + H
        last = t == RO - 1
        kt, rf, pc = v("KP", M * t + own + a, M * t + own + b), v("rfT", a, b), v("pc%d" % h, 0, H)
        ge, sg = v("ge", a, b), v("sg", a, b)
        cur[0] = "e%d" % h
        ts(ge, pc, col(cTH), 2.0, A.is_ge, A.mult)
        mm(v("pS", 0, H), v("BO"), ge, True, True)
        ts(sg, v("pS", 0, H), col(cSG), 2.0, A.is_lt, A.mult)
        if last:
            tt(v("pw", 0, H), sg, v("t1", a, b), A.mult)
            tt(v("yb", a, b), v("pw", 0, H), v("t4", a, b), A.add)
            dma("Y", T.yo[:, a:b], T.yb[:, a:b], rg(v("yb", a, b)), [])
        else:
            mm(v("pS", H, 2 * H), v("Q3", 0, 128), ge, True, False)
            mm(v("pS", H, 2 * H), v("Q3", 128, 256), rf, False, False)
            mm(v("pS", H, 2 * H), v("Q3", 256, 384), sg, False, True)
            if CFG["q"] == "V":
                ts(v("q", a, b), v("pS", H, 2 * H), 1.0, None, A.add)
            else:
                act(v("q", a, b), v("pS", H, 2 * H), AF.Identity, 1.0, 1.0)
            mm(v("pw", L + a, L + b), v("E", 128 * (t + 1), 128 * (t + 2)), v("one", a, b), True, True)
            for j in range(16):
                mm(v("pw", 0, 8), v("Fw", 15 - j, 143 - j), v("q", a + j, b, step=16), j == 0, j == 15)
            c = 16 * (t + 1) + 8 * h
            tt(v("w3", 8 * h, 8 * h + 8), v("pw", 0, 8), v("BT2", c, c + 8), A.add)
            ts(v("w4", 8 * h, 8 * h + 8), v("w3", 8 * h, 8 * h + 8), M - 1, None, A.bitwise_and)
            cp(v("ou", 8 * h, 8 * h + 8), v("w4", 8 * h, 8 * h + 8))
            cur[0] = "u%d" % h
            up = v("pU", 0, H)
            mm(up, v("M8"), rf, True, False)
            mm(up, v("D", 128 * t, 128 * t + 128), v("one", a, b), False, False)
            mm(up, v("Id"), v("Bn", a, b), False, False)
            mm(up, v("M8"), sg, False, True)
            n, e = L * (t + 1), M * (t + 1) + own
            tt(v("KS", n + a, n + b), up, kt, A.max)
            share_half(CFG["splitk"], h, "KS", n, "KK", M * (t + 1))
            if h == 0:
                dma("Y", T.KK[:, e:e + L], T.KS[:, n:n + L], rg(v("KS", n, n + L)), rg(v("KK", e, e + L)))
        cur[0] = "r"
        mm(v("pU", L, L + H, 8), v("Sel", 0, 8), rf, True, False)
        mm(v("pU", L, L + H, 8), v("Sel", 8, 16), sg, False, True)
        act(v("Ro", t * L + a, t * L + b, 8), v("pU", L, L + H, 8), AF.Identity, -128.0, 1.0)
        if last or h == 0:
            c, d = (t * L + a, t * L + b) if last else (t * L, t * L + L)
            dma("S" if last else "Y", T.yr[:, c:d], T.Ro[0:8, c:d], rg(v("Ro", c, d)), [])

    for t in range(RO):
        front(t, 1)
        if t > 0:
            close(t - 1, 0)
        front(t, 0)
        counts(t, 1)
        counts(t, 0)
        back(t, 1)
        back(t, 0)
        close(t, 1)
    close(RO - 1, 0)
    emit(g, T, ops)
